import numpy as np, ml_dtypes
CORES = [10,14,66,70,74,78,82,86,90,94,106,110]
N = 12
VB, TK = 4, 128
def setup_inputs(rng):
    h = rng.standard_normal((128, TK), dtype=np.float32) / 4; w = rng.standard_normal((N, 128, VB * 128), dtype=np.float32)
    a = 2 * np.pi * rng.random((TK)); s = 400 * rng.random((TK)) ** 1.5; h[0] = s * np.cos(a); h[1] = s * np.sin(a); h[2] = 150 * rng.standard_normal((TK)); w[:, 2, :] = 1 + w[:, 2, :] / 50
    a = (2 * np.pi * rng.random() + np.pi / 2 * (rng.permutation(N).reshape(N, 1, 1) + 0.5) / N - 0.5 + (np.arange(VB).reshape(1, VB, 1) + rng.random((N, VB, 128))) / VB).reshape(N, VB * 128); w[:, 0, :] = np.cos(a); w[:, 1, :] = np.sin(a)
    tgt = rng.integers(0, N * VB * 128, size=TK)
    oh = np.zeros((N * VB * 128, TK), np.float32); oh[tgt, np.arange(TK)] = 1.0
    oh = oh.reshape(N, VB, 128, TK).transpose(0, 2, 1, 3).reshape(N, 128, VB * TK)
    return {"h": np.broadcast_to(h, (N, 128, TK)).astype(ml_dtypes.bfloat16), "w": w.astype(ml_dtypes.bfloat16), "oh": oh.astype(ml_dtypes.bfloat16)}
def reference(h, w, oh):
    H, W, OH = h.astype(np.float64), w.astype(np.float64), oh.astype(np.float64)
    Z = np.concatenate([W[r].T @ H[r] for r in range(N)], axis=0)
    O = np.concatenate([OH[r][:, TK * b:TK * b + TK] for r in range(N) for b in range(VB)], axis=0)
    m = Z.max(axis=0)
    l = m + np.log(np.exp(Z - m).sum(axis=0)) - (O * Z).sum(axis=0)
    return {"l": np.broadcast_to(l.astype(np.float32), (N, 1, TK))}

@@ -1,0 +1,161 @@
+import math
+from concourse.bass import DstId, RemoteDMATransfer
+from concourse.mybir import AluOpType, AxisListType, ActivationFunctionType
+
+N = 12
+TK = 128
+VB = 4
+K = 128
+D = math.log(6400.0) / K
+NENG = 4
+
+SCRATCH = {
+    "h_sb": ("sbuf", [128, TK], "bfloat16"),
+    "w_sb": ("sbuf", [128, VB * 128], "bfloat16"),
+    "oh_sb": ("sbuf", [128, VB * TK], "bfloat16"),
+    "zT": ("psum", [128, 512], "float32"),
+    "zb": ("psum", [128, 512], "float32"),
+    "tp": ("psum", [128, 512], "float32"),
+    "p1": ("psum", [128, 512], "float32"),
+    "p2": ("psum", [128, 512], "float32"),
+    "p3": ("psum", [128, 512], "float32"),
+    "prod": ("sbuf", [128, VB * TK], "float32"),
+    "esc": ("sbuf", [128, 512], "float32"),
+    "ones": ("sbuf", [128, 4], "float32"),
+    "idn": ("sbuf", [128, N], "float32"),
+    "iot": ("sbuf", [128, K], "float32"),
+    "thr": ("sbuf", [128, K], "float32"),
+    "sgn": ("sbuf", [128, K], "float32"),
+    "stat": ("sbuf", [128, 4], "float32"),
+    "land": ("dram", [N, 128, 3], "float32"),
+    "tab": ("sbuf", [128, 3 * TK], "float32"),
+    "nmn": ("sbuf", [128, 4], "float32"),
+    "ee": ("sbuf", [128, N], "float32"),
+    "pp": ("sbuf", [128, N], "float32"),
+    "ssum": ("sbuf", [128, 4], "float32"),
+    "cnt": ("sbuf", [128, 4], "float32"),
+    "uu": ("sbuf", [128, 4], "float32"),
+    "b1": ("sbuf", [128, 4], "float32"),
+    "rr": ("sbuf", [128, 4], "float32"),
+    "lcol": ("sbuf", [128, 4], "float32"),
+}
+SEMAPHORES = ["ld_h", "ld_w", "ld_oh", "c_iota", "c_thr", "c_ones", "c_idn0", "c_idn", "mm1", "mm2", "vmax", "aexp",
+              "vp0", "vp1", "vp2", "vp3", "mm3", "vt", "d1", "arr", "sent", "d2", "t1", "t2", "t3", "v1", "a1", "vb",
+              "v2", "v3", "a2", "a3", "v6", "v7", "d3"]
+
+
+def _hops(topo, a, b):
+    ca, cb = topo.chip(a), topo.chip(b)
+    if ca == cb:
+        return 0
+    return 1 if (topo.mates(ca, cb) or topo.same_plane(ca, cb)) else 2
+
+
+def rank_program(g, core, T, topo):
+    rank = T.rank_of(core)
+    if rank is None:
+        return
+    s = T.sem
+    pe, v, a, sy = g.tensor, g.vector, g.scalar, g.sync
+    ALU, ACT, AX = AluOpType, ActivationFunctionType, AxisListType.X
+
+    a.dma_start(T.h_sb[:], T.h[:]).then_inc(s.ld_h, 16)
+    sy.dma_start(T.w_sb[:], T.w[:]).then_inc(s.ld_w, 16)
+    sy.dma_start(T.oh_sb[:], T.oh[:]).then_inc(s.ld_oh, 16)
+
+    g.iota(T.iot[:], [[1, K]], 1, 0, allow_small_or_imprecise_dtypes=True).then_inc(s.c_iota, 1)
+    a.wait_ge(s.c_iota, 1)
+    a.activation(T.thr[:], T.iot[:], ACT.Exp, scale=D).then_inc(s.c_thr, 1)
+    v.memset(T.ones[:], 1.0).then_inc(s.c_ones, 1)
+    v.memset(T.idn[0:N, :], 1.0).then_inc(s.c_idn0, 1)
+    g.wait_ge(s.c_idn0, 1)
+    g.affine_select(T.idn[0:N, :], T.idn[0:N, :], [[-1, N]], ALU.is_equal, 0.0, 0, 1).then_inc(s.c_idn, 1)
+
+    pe.wait_ge(s.ld_h, 16)
+    pe.wait_ge(s.ld_w, 16)
+    pe.matmul(T.zT[:], T.h_sb[:], T.w_sb[:], True, True).then_inc(s.mm1, 1)
+    for b in range(VB):
+        blk = slice(128 * b, 128 * b + 128)
+        pe.matmul(T.zb[:, blk], T.w_sb[:, blk], T.h_sb[:], True, True).then_inc(s.mm2, 1)
+
+    v.wait_ge(s.mm1, 1)
+    v.tensor_reduce(T.stat[:, 0:1], T.zT[:], AX, ALU.max, negate=True).then_inc(s.vmax, 1)
+    a.wait_ge(s.vmax, 1)
+    a.activation(T.esc[:], T.zT[:], ACT.Exp, bias=T.stat[:, 0:1], scale=1.0,
+                 accum_out=T.stat[:, 1:2]).then_inc(s.aexp, 1)
+
+    v.wait_ge(s.mm2, VB)
+    v.wait_ge(s.ld_oh, 16)
+    pe.wait_ge(s.c_ones, 1)
+    for b in range(VB):
+        blk = slice(128 * b, 128 * b + 128)
+        v.tensor_tensor(T.prod[:, blk], T.zb[:, blk], T.oh_sb[:, blk], ALU.mult).then_inc(s["vp%d" % b], 1)
+        pe.wait_ge(s["vp%d" % b], 1)
+        mm = pe.matmul(T.tp[:, 0:1], T.prod[:, blk], T.ones[:, 0:1], b == 0, b == VB - 1)
+    mm.then_inc(s.mm3, 1)
+    v.wait_ge(s.mm3, 1)
+    v.tensor_copy(T.stat[:, 2:3], T.tp[:, 0:1]).then_inc(s.vt, 1)
+
+    sy.wait_ge(s.aexp, 1)
+    sy.wait_ge(s.vt, 1)
+    sy.dma_start(T.land[rank], T.stat[:, 0:3]).then_inc(s.d1, 16)
+
+    dests = sorted([c for c in T.cores if c != core], key=lambda c: -_hops(topo, core, c))
+    allowed = -1
+    for c in dests:
+        assert topo.may_write(core, c)
+        allowed &= topo.mask(core, c)
+    engines = [e for e in range(16) if (allowed >> e) & 1]
+    engines = engines[::len(engines) // NENG][:NENG]
+    transfers = []
+    for i, e in enumerate(engines):
+        mine = dests[i::NENG]
+        ids = []
+        for c in mine:
+            rid, pid, _se = topo.addr(c)
+            ids.append(DstId(rid=rid, pnc=pid))
+        transfers.append(RemoteDMATransfer(dst_ids=ids, dma_engine_mask=1 << e, remote_sem=s.arr,
+                                           srcs=[T.land[rank]], dsts=[T.land[rank] for _c in mine], alu_op=0))
+    g.wait_ge(s.d1, 16)
+    g.remote_dma_fused(transfers, local_sem=s.sent)
+
+    sy.wait_ge(s.d1, 16)
+    sy.wait_ge(s.arr, N - 1)
+    sy.dma_start(T.tab[0:N, :], T.land[:]).then_inc(s.d2, 16)
+    pe.wait_ge(s.d2, 16)
+    pe.wait_ge(s.c_idn, 1)
+    pe.transpose(T.p1[:, 0:N], T.tab[0:N, 0:3 * TK:3], T.idn[0:N, :]).then_inc(s.t1, 1)
+    pe.transpose(T.p2[:, 0:N], T.tab[0:N, 1:3 * TK:3], T.idn[0:N, :]).then_inc(s.t2, 1)
+    pe.matmul(T.p3[:, 0:1], T.tab[0:N, 2:3 * TK:3], T.ones[0:N, 0:1], True, True).then_inc(s.t3, 1)
+
+    const = D * (K + 1) / 2 - 1.0 - D * D / 16
+    v.wait_ge(s.t1, 1)
+    v.tensor_reduce(T.nmn[:, 0:1], T.p1[:, 0:N], AX, ALU.min).then_inc(s.v1, 1)
+    a.wait_ge(s.v1, 1)
+    a.activation(T.ee[:], T.p1[:, 0:N], ACT.Exp, bias=T.nmn[:, 0:1], scale=-1.0).then_inc(s.a1, 1)
+    v.wait_ge(s.v1, 1)
+    v.wait_ge(s.t3, 1)
+    v.tensor_scalar(T.b1[:, 0:1], T.p3[:, 0:1], T.nmn[:, 0:1], -const, ALU.add, ALU.add).then_inc(s.vb, 1)
+    v.wait_ge(s.a1, 1)
+    v.wait_ge(s.t2, 1)
+    v.tensor_tensor(T.pp[:], T.ee[:], T.p2[:, 0:N], ALU.mult).then_inc(s.v2, 1)
+    v.wait_ge(s.v2, 1)
+    v.tensor_reduce(T.ssum[:, 0:1], T.pp[:], AX, ALU.add).then_inc(s.v3, 1)
+    a.wait_ge(s.v3, 1)
+    a.wait_ge(s.c_thr, 1)
+    a.activation(T.sgn[:], T.thr[:], ACT.Sign, bias=T.ssum[:, 0:1], scale=-1.0,
+                 accum_out=T.cnt[:, 0:1]).then_inc(s.a2, 1)
+    a.wait_ge(s.a2, 1)
+    a.activation(T.uu[:, 0:1], T.cnt[:, 0:1], ACT.Exp, bias=-D * (K + 1) / 2, scale=-D / 2).then_inc(s.a3, 1)
+    v.wait_ge(s.a2, 1)
+    v.wait_ge(s.vb, 1)
+    v.tensor_scalar(T.rr[:, 0:1], T.cnt[:, 0:1], D / 2, T.b1[:, 0:1], ALU.mult, ALU.subtract).then_inc(s.v6, 1)
+    v.wait_ge(s.a3, 1)
+    v.wait_ge(s.v6, 1)
+    v.wait_ge(s.v3, 1)
+    v.tensor_scalar(T.lcol[:, 0:1], T.uu[:, 0:1], T.ssum[:, 0:1], T.rr[:, 0:1], ALU.mult, ALU.add).then_inc(s.v7, 1)
+
+    sy.wait_ge(s.v7, 1)
+    sy.dma_start(T.l[:], T.lcol[:, 0:1]).then_inc(s.d3, 16)
+    sy.wait_ge(s.d3, 16)
+    g.wait_ge(s.sent, NENG)

@@ -14,21 +14,28 @@ SCRATCH = {
     "w_sb": ("sbuf", [128, VB * 128], "bfloat16"),
     "oh_sb": ("sbuf", [128, VB * TK], "bfloat16"),
     "zT": ("psum", [128, 512], "float32"),
-    "zb": ("psum", [128, 512], "float32"),
-    "tp": ("psum", [128, 512], "float32"),
+    "bkA": ("psum", [128, 1024], "bfloat16"),
+    "bkB": ("psum", [128, 1024], "bfloat16"),
+    "U": ("psum", [128, 512], "float32"),
     "p1": ("psum", [128, 512], "float32"),
     "p2": ("psum", [128, 512], "float32"),
     "p3": ("psum", [128, 512], "float32"),
-    "prod": ("sbuf", [128, VB * TK], "float32"),
+    "hT": ("sbuf", [128, 128], "bfloat16"),
+    "wT": ("sbuf", [128, VB * 128], "bfloat16"),
+    "q": ("sbuf", [128, 128], "float32"),
     "esc": ("sbuf", [128, 512], "float32"),
     "ones": ("sbuf", [128, 4], "float32"),
     "idn": ("sbuf", [128, N], "float32"),
+    "idb": ("sbuf", [128, 128], "bfloat16"),
     "iot": ("sbuf", [128, K], "float32"),
     "thr": ("sbuf", [128, K], "float32"),
     "sgn": ("sbuf", [128, K], "float32"),
-    "stat": ("sbuf", [128, 4], "float32"),
-    "land": ("dram", [N, 128, 3], "float32"),
-    "tab": ("sbuf", [128, 3 * TK], "float32"),
+    "sta": ("sbuf", [128, 4], "float32"),
+    "stb": ("sbuf", [128, 4], "float32"),
+    "la": ("dram", [N, 128, 1], "float32"),
+    "lb": ("dram", [N, 128, 2], "float32"),
+    "ta": ("sbuf", [128, TK], "float32"),
+    "tb": ("sbuf", [128, 2 * TK], "float32"),
     "nmn": ("sbuf", [128, 4], "float32"),
     "ee": ("sbuf", [128, N], "float32"),
     "pp": ("sbuf", [128, N], "float32"),
@@ -39,8 +46,9 @@ SCRATCH = {
     "rr": ("sbuf", [128, 4], "float32"),
     "lcol": ("sbuf", [128, 4], "float32"),
 }
-SEMAPHORES = ["ld_h", "ld_w", "ld_oh", "c_iota", "c_thr", "c_ones", "c_idn0", "c_idn", "mm1", "mm2", "vmax", "aexp",
-              "vp0", "vp1", "vp2", "vp3", "mm3", "vt", "d1", "arr", "sent", "d2", "t1", "t2", "t3", "v1", "a1", "vb",
+SEMAPHORES = ["ld_h", "ld_w", "ld_oh", "c_iota", "c_thr", "c_ones", "c_idn0", "c_idn", "c_idb0", "c_idb",
+              "tH", "vh", "mm1", "tA", "tB", "acA", "vcb", "mmU", "vq", "vt", "vmax", "aexp",
+              "d1a", "d1b", "arr_a", "arr_b", "sent", "d2a", "d2b", "t1", "t2", "t3", "v1", "a1", "vb",
               "v2", "v3", "a2", "a3", "v6", "v7", "d3"]
 
 
@@ -59,47 +67,6 @@ def rank_program(g, core, T, topo):
     pe, v, a, sy = g.tensor, g.vector, g.scalar, g.sync
     ALU, ACT, AX = AluOpType, ActivationFunctionType, AxisListType.X
 
-    a.dma_start(T.h_sb[:], T.h[:]).then_inc(s.ld_h, 16)
-    sy.dma_start(T.w_sb[:], T.w[:]).then_inc(s.ld_w, 16)
-    sy.dma_start(T.oh_sb[:], T.oh[:]).then_inc(s.ld_oh, 16)
-
-    g.iota(T.iot[:], [[1, K]], 1, 0, allow_small_or_imprecise_dtypes=True).then_inc(s.c_iota, 1)
-    a.wait_ge(s.c_iota, 1)
-    a.activation(T.thr[:], T.iot[:], ACT.Exp, scale=D).then_inc(s.c_thr, 1)
-    v.memset(T.ones[:], 1.0).then_inc(s.c_ones, 1)
-    v.memset(T.idn[0:N, :], 1.0).then_inc(s.c_idn0, 1)
-    g.wait_ge(s.c_idn0, 1)
-    g.affine_select(T.idn[0:N, :], T.idn[0:N, :], [[-1, N]], ALU.is_equal, 0.0, 0, 1).then_inc(s.c_idn, 1)
-
-    pe.wait_ge(s.ld_h, 16)
-    pe.wait_ge(s.ld_w, 16)
-    pe.matmul(T.zT[:], T.h_sb[:], T.w_sb[:], True, True).then_inc(s.mm1, 1)
-    for b in range(VB):
-        blk = slice(128 * b, 128 * b + 128)
-        pe.matmul(T.zb[:, blk], T.w_sb[:, blk], T.h_sb[:], True, True).then_inc(s.mm2, 1)
-
-    v.wait_ge(s.mm1, 1)
-    v.tensor_reduce(T.stat[:, 0:1], T.zT[:], AX, ALU.max, negate=True).then_inc(s.vmax, 1)
-    a.wait_ge(s.vmax, 1)
-    a.activation(T.esc[:], T.zT[:], ACT.Exp, bias=T.stat[:, 0:1], scale=1.0,
-                 accum_out=T.stat[:, 1:2]).then_inc(s.aexp, 1)
-
-    v.wait_ge(s.mm2, VB)
-    v.wait_ge(s.ld_oh, 16)
-    pe.wait_ge(s.c_ones, 1)
-    for b in range(VB):
-        blk = slice(128 * b, 128 * b + 128)
-        v.tensor_tensor(T.prod[:, blk], T.zb[:, blk], T.oh_sb[:, blk], ALU.mult).then_inc(s["vp%d" % b], 1)
-        pe.wait_ge(s["vp%d" % b], 1)
-        mm = pe.matmul(T.tp[:, 0:1], T.prod[:, blk], T.ones[:, 0:1], b == 0, b == VB - 1)
-    mm.then_inc(s.mm3, 1)
-    v.wait_ge(s.mm3, 1)
-    v.tensor_copy(T.stat[:, 2:3], T.tp[:, 0:1]).then_inc(s.vt, 1)
-
-    sy.wait_ge(s.aexp, 1)
-    sy.wait_ge(s.vt, 1)
-    sy.dma_start(T.land[rank], T.stat[:, 0:3]).then_inc(s.d1, 16)
-
     dests = sorted([c for c in T.cores if c != core], key=lambda c: -_hops(topo, core, c))
     allowed = -1
     for c in dests:
@@ -107,35 +74,103 @@ def rank_program(g, core, T, topo):
         allowed &= topo.mask(core, c)
     engines = [e for e in range(16) if (allowed >> e) & 1]
     engines = engines[::len(engines) // NENG][:NENG]
-    transfers = []
-    for i, e in enumerate(engines):
-        mine = dests[i::NENG]
-        ids = []
-        for c in mine:
-            rid, pid, _se = topo.addr(c)
-            ids.append(DstId(rid=rid, pnc=pid))
-        transfers.append(RemoteDMATransfer(dst_ids=ids, dma_engine_mask=1 << e, remote_sem=s.arr,
-                                           srcs=[T.land[rank]], dsts=[T.land[rank] for _c in mine], alu_op=0))
-    g.wait_ge(s.d1, 16)
-    g.remote_dma_fused(transfers, local_sem=s.sent)
 
-    sy.wait_ge(s.d1, 16)
-    sy.wait_ge(s.arr, N - 1)
-    sy.dma_start(T.tab[0:N, :], T.land[:]).then_inc(s.d2, 16)
-    pe.wait_ge(s.d2, 16)
+    def exchange(slot, sem):
+        transfers = []
+        for i, e in enumerate(engines):
+            mine = dests[i::NENG]
+            ids = []
+            for c in mine:
+                rid, pid, _se = topo.addr(c)
+                ids.append(DstId(rid=rid, pnc=pid))
+            transfers.append(RemoteDMATransfer(dst_ids=ids, dma_engine_mask=1 << e, remote_sem=sem,
+                                               srcs=[slot], dsts=[slot for _c in mine], alu_op=0))
+        g.remote_dma_fused(transfers, local_sem=s.sent)
+
+    a.dma_start(T.h_sb[:], T.h[:]).then_inc(s.ld_h, 16)
+    sy.dma_start(T.w_sb[:], T.w[:]).then_inc(s.ld_w, 16)
+    sy.dma_start(T.oh_sb[:], T.oh[:]).then_inc(s.ld_oh, 16)
+
+    v.memset(T.idb[:], 1.0).then_inc(s.c_idb0, 1)
+    v.memset(T.idn[0:N, :], 1.0).then_inc(s.c_idn0, 1)
+    v.memset(T.ones[:], 1.0).then_inc(s.c_ones, 1)
+    g.iota(T.iot[:], [[1, K]], 1, 0, allow_small_or_imprecise_dtypes=True).then_inc(s.c_iota, 1)
+    a.wait_ge(s.c_iota, 1)
+    a.activation(T.thr[:], T.iot[:], ACT.Exp, scale=D).then_inc(s.c_thr, 1)
+    g.wait_ge(s.c_idb0, 1)
+    g.affine_select(T.idb[:], T.idb[:], [[-1, 128]], ALU.is_equal, 0.0, 0, 1).then_inc(s.c_idb, 1)
+    g.wait_ge(s.c_idn0, 1)
+    g.affine_select(T.idn[0:N, :], T.idn[0:N, :], [[-1, N]], ALU.is_equal, 0.0, 0, 1).then_inc(s.c_idn, 1)
+
+    pe.wait_ge(s.ld_h, 16)
+    pe.wait_ge(s.c_idb, 1)
+    pe.transpose(T.bkA[:, 0:128], T.h_sb[:], T.idb[:]).then_inc(s.tH, 1)
+    pe.wait_ge(s.ld_w, 16)
+    pe.matmul(T.zT[:], T.h_sb[:], T.w_sb[:], True, True).then_inc(s.mm1, 1)
+    pe.wait_ge(s.vh, 1)
+    pe.transpose(T.bkA[:, 128:256], T.w_sb[:, 0:128], T.idb[:]).then_inc(s.tA, 1)
+    pe.transpose(T.bkA[:, 256:384], T.w_sb[:, 128:256], T.idb[:]).then_inc(s.tA, 1)
+    pe.transpose(T.bkB[:, 0:128], T.w_sb[:, 256:384], T.idb[:]).then_inc(s.tB, 1)
+    pe.transpose(T.bkB[:, 128:256], T.w_sb[:, 384:512], T.idb[:]).then_inc(s.tB, 1)
+
+    v.wait_ge(s.tH, 1)
+    v.tensor_copy(T.hT[:], T.bkA[:, 0:128]).then_inc(s.vh, 1)
+
+    v.wait_ge(s.mm1, 1)
+    v.tensor_reduce(T.sta[:, 0:1], T.zT[:], AX, ALU.max, negate=True).then_inc(s.vmax, 1)
+    sy.wait_ge(s.vmax, 1)
+    sy.dma_start(T.la[rank], T.sta[:, 0:1]).then_inc(s.d1a, 16)
+    g.wait_ge(s.d1a, 16)
+    exchange(T.la[rank], s.arr_a)
+
+    a.wait_ge(s.tA, 2)
+    a.activation(T.wT[:, 0:256], T.bkA[:, 128:384], ACT.Copy).then_inc(s.acA, 1)
+    v.wait_ge(s.tB, 2)
+    v.tensor_copy(T.wT[:, 256:512], T.bkB[:, 0:256]).then_inc(s.vcb, 1)
+
+    a.wait_ge(s.vmax, 1)
+    a.activation(T.esc[:], T.zT[:], ACT.Exp, bias=T.sta[:, 0:1], scale=1.0,
+                 accum_out=T.stb[:, 0:1]).then_inc(s.aexp, 1)
+
+    pe.wait_ge(s.ld_oh, 16)
+    pe.wait_ge(s.acA, 1)
+    pe.matmul(T.U[:, 0:128], T.oh_sb[:, 0:128], T.wT[:, 0:128], True, False)
+    pe.matmul(T.U[:, 0:128], T.oh_sb[:, 128:256], T.wT[:, 128:256], False, False)
+    pe.wait_ge(s.vcb, 1)
+    pe.matmul(T.U[:, 0:128], T.oh_sb[:, 256:384], T.wT[:, 256:384], False, False)
+    pe.matmul(T.U[:, 0:128], T.oh_sb[:, 384:512], T.wT[:, 384:512], False, True).then_inc(s.mmU, 1)
+    v.wait_ge(s.mmU, 1)
+    v.wait_ge(s.vh, 1)
+    v.tensor_tensor(T.q[:], T.U[:, 0:128], T.hT[:], ALU.mult).then_inc(s.vq, 1)
+    v.wait_ge(s.vq, 1)
+    v.tensor_reduce(T.stb[:, 1:2], T.q[:], AX, ALU.add).then_inc(s.vt, 1)
+
+    sy.wait_ge(s.aexp, 1)
+    sy.wait_ge(s.vt, 1)
+    sy.dma_start(T.lb[rank], T.stb[:, 0:2]).then_inc(s.d1b, 16)
+    g.wait_ge(s.d1b, 16)
+    exchange(T.lb[rank], s.arr_b)
+
+    a.wait_ge(s.d1a, 16)
+    a.wait_ge(s.arr_a, N - 1)
+    a.dma_start(T.ta[0:N, :], T.la[:]).then_inc(s.d2a, 16)
+    pe.wait_ge(s.d2a, 16)
     pe.wait_ge(s.c_idn, 1)
-    pe.transpose(T.p1[:, 0:N], T.tab[0:N, 0:3 * TK:3], T.idn[0:N, :]).then_inc(s.t1, 1)
-    pe.transpose(T.p2[:, 0:N], T.tab[0:N, 1:3 * TK:3], T.idn[0:N, :]).then_inc(s.t2, 1)
-    pe.matmul(T.p3[:, 0:1], T.tab[0:N, 2:3 * TK:3], T.ones[0:N, 0:1], True, True).then_inc(s.t3, 1)
-
-    const = D * (K + 1) / 2 - 1.0 - D * D / 16
+    pe.transpose(T.p1[:, 0:N], T.ta[0:N, :], T.idn[0:N, :]).then_inc(s.t1, 1)
     v.wait_ge(s.t1, 1)
     v.tensor_reduce(T.nmn[:, 0:1], T.p1[:, 0:N], AX, ALU.min).then_inc(s.v1, 1)
     a.wait_ge(s.v1, 1)
     a.activation(T.ee[:], T.p1[:, 0:N], ACT.Exp, bias=T.nmn[:, 0:1], scale=-1.0).then_inc(s.a1, 1)
-    v.wait_ge(s.v1, 1)
-    v.wait_ge(s.t3, 1)
-    v.tensor_scalar(T.b1[:, 0:1], T.p3[:, 0:1], T.nmn[:, 0:1], -const, ALU.add, ALU.add).then_inc(s.vb, 1)
+
+    sy.wait_ge(s.d1b, 16)
+    sy.wait_ge(s.arr_b, N - 1)
+    sy.dma_start(T.tb[0:N, :], T.lb[:]).then_inc(s.d2b, 16)
+    pe.wait_ge(s.d2b, 16)
+    pe.wait_ge(s.c_ones, 1)
+    pe.transpose(T.p2[:, 0:N], T.tb[0:N, 0:2 * TK:2], T.idn[0:N, :]).then_inc(s.t2, 1)
+    pe.matmul(T.p3[:, 0:1], T.tb[0:N, 1:2 * TK:2], T.ones[0:N, 0:1], True, True).then_inc(s.t3, 1)
+
+    const = D * (K + 1) / 2 - 1.0 - D * D / 16
     v.wait_ge(s.a1, 1)
     v.wait_ge(s.t2, 1)
     v.tensor_tensor(T.pp[:], T.ee[:], T.p2[:, 0:N], ALU.mult).then_inc(s.v2, 1)
@@ -147,6 +182,9 @@ def rank_program(g, core, T, topo):
                  accum_out=T.cnt[:, 0:1]).then_inc(s.a2, 1)
     a.wait_ge(s.a2, 1)
     a.activation(T.uu[:, 0:1], T.cnt[:, 0:1], ACT.Exp, bias=-D * (K + 1) / 2, scale=-D / 2).then_inc(s.a3, 1)
+    v.wait_ge(s.v1, 1)
+    v.wait_ge(s.t3, 1)
+    v.tensor_scalar(T.b1[:, 0:1], T.p3[:, 0:1], T.nmn[:, 0:1], -const, ALU.add, ALU.add).then_inc(s.vb, 1)
     v.wait_ge(s.a2, 1)
     v.wait_ge(s.vb, 1)
     v.tensor_scalar(T.rr[:, 0:1], T.cnt[:, 0:1], D / 2, T.b1[:, 0:1], ALU.mult, ALU.subtract).then_inc(s.v6, 1)
@@ -158,4 +196,4 @@ def rank_program(g, core, T, topo):
     sy.wait_ge(s.v7, 1)
     sy.dma_start(T.l[:], T.lcol[:, 0:1]).then_inc(s.d3, 16)
     sy.wait_ge(s.d3, 16)
-    g.wait_ge(s.sent, NENG)
+    g.wait_ge(s.sent, 2 * NENG)

import math
from concourse.bass import DstId, RemoteDMATransfer
from concourse.mybir import AluOpType, AxisListType, ActivationFunctionType

N = 12
TK = 128
VB = 4
K = 128
D = math.log(6400.0) / K
NENG = 4

SCRATCH = {
    "h_sb": ("sbuf", [128, TK], "bfloat16"),
    "w_sb": ("sbuf", [128, VB * 128], "bfloat16"),
    "oh_sb": ("sbuf", [128, VB * TK], "bfloat16"),
    "zT": ("psum", [128, 512], "float32"),
    "bkA": ("psum", [128, 1024], "bfloat16"),
    "bkB": ("psum", [128, 1024], "bfloat16"),
    "U": ("psum", [128, 512], "float32"),
    "p1": ("psum", [128, 512], "float32"),
    "p2": ("psum", [128, 512], "float32"),
    "p3": ("psum", [128, 512], "float32"),
    "hT": ("sbuf", [128, 128], "bfloat16"),
    "wT": ("sbuf", [128, VB * 128], "bfloat16"),
    "q": ("sbuf", [128, 128], "float32"),
    "esc": ("sbuf", [128, 512], "float32"),
    "ones": ("sbuf", [128, 4], "float32"),
    "idn": ("sbuf", [128, N], "float32"),
    "idb": ("sbuf", [128, 128], "bfloat16"),
    "iot": ("sbuf", [128, K], "float32"),
    "thr": ("sbuf", [128, K], "float32"),
    "sgn": ("sbuf", [128, K], "float32"),
    "sta": ("sbuf", [128, 4], "float32"),
    "stb": ("sbuf", [128, 4], "float32"),
    "la": ("dram", [N, 128, 1], "float32"),
    "lb": ("dram", [N, 128, 2], "float32"),
    "ta": ("sbuf", [128, TK], "float32"),
    "tb": ("sbuf", [128, 2 * TK], "float32"),
    "nmn": ("sbuf", [128, 4], "float32"),
    "ee": ("sbuf", [128, N], "float32"),
    "pp": ("sbuf", [128, N], "float32"),
    "ssum": ("sbuf", [128, 4], "float32"),
    "cnt": ("sbuf", [128, 4], "float32"),
    "uu": ("sbuf", [128, 4], "float32"),
    "b1": ("sbuf", [128, 4], "float32"),
    "rr": ("sbuf", [128, 4], "float32"),
    "lcol": ("sbuf", [128, 4], "float32"),
}
SEMAPHORES = ["ld_h", "ld_w", "ld_oh", "c_iota", "c_thr", "c_ones", "c_idn0", "c_idn", "c_idb0", "c_idb",
              "tH", "vh", "mm1", "tA", "tB", "acA", "vcb", "mmU", "vq", "vt", "vmax", "aexp",
              "d1a", "d1b", "arr_a", "arr_b", "sent", "d2a", "d2b", "t1", "t2", "t3", "v1", "a1", "vb",
              "v2", "v3", "a2", "a3", "v6", "v7", "d3"]


def _hops(topo, a, b):
    ca, cb = topo.chip(a), topo.chip(b)
    if ca == cb:
        return 0
    return 1 if (topo.mates(ca, cb) or topo.same_plane(ca, cb)) else 2


def rank_program(g, core, T, topo):
    rank = T.rank_of(core)
    if rank is None:
        return
    s = T.sem
    pe, v, a, sy = g.tensor, g.vector, g.scalar, g.sync
    ALU, ACT, AX = AluOpType, ActivationFunctionType, AxisListType.X

    dests = sorted([c for c in T.cores if c != core], key=lambda c: -_hops(topo, core, c))
    allowed = -1
    for c in dests:
        assert topo.may_write(core, c)
        allowed &= topo.mask(core, c)
    engines = [e for e in range(16) if (allowed >> e) & 1]
    engines = engines[::len(engines) // NENG][:NENG]

    def exchange(slot, sem):
        transfers = []
        for i, e in enumerate(engines):
            mine = dests[i::NENG]
            ids = []
            for c in mine:
                rid, pid, _se = topo.addr(c)
                ids.append(DstId(rid=rid, pnc=pid))
            transfers.append(RemoteDMATransfer(dst_ids=ids, dma_engine_mask=1 << e, remote_sem=sem,
                                               srcs=[slot], dsts=[slot for _c in mine], alu_op=0))
        g.remote_dma_fused(transfers, local_sem=s.sent)

    a.dma_start(T.h_sb[:], T.h[:]).then_inc(s.ld_h, 16)
    sy.dma_start(T.w_sb[:], T.w[:]).then_inc(s.ld_w, 16)
    sy.dma_start(T.oh_sb[:], T.oh[:]).then_inc(s.ld_oh, 16)

    v.memset(T.idb[:], 1.0).then_inc(s.c_idb0, 1)
    v.memset(T.idn[0:N, :], 1.0).then_inc(s.c_idn0, 1)
    v.memset(T.ones[:], 1.0).then_inc(s.c_ones, 1)
    g.iota(T.iot[:], [[1, K]], 1, 0, allow_small_or_imprecise_dtypes=True).then_inc(s.c_iota, 1)
    a.wait_ge(s.c_iota, 1)
    a.activation(T.thr[:], T.iot[:], ACT.Exp, scale=D).then_inc(s.c_thr, 1)
    g.wait_ge(s.c_idb0, 1)
    g.affine_select(T.idb[:], T.idb[:], [[-1, 128]], ALU.is_equal, 0.0, 0, 1).then_inc(s.c_idb, 1)
    g.wait_ge(s.c_idn0, 1)
    g.affine_select(T.idn[0:N, :], T.idn[0:N, :], [[-1, N]], ALU.is_equal, 0.0, 0, 1).then_inc(s.c_idn, 1)

    pe.wait_ge(s.ld_h, 16)
    pe.wait_ge(s.c_idb, 1)
    pe.transpose(T.bkA[:, 0:128], T.h_sb[:], T.idb[:]).then_inc(s.tH, 1)
    pe.wait_ge(s.ld_w, 16)
    pe.matmul(T.zT[:], T.h_sb[:], T.w_sb[:], True, True).then_inc(s.mm1, 1)
    pe.wait_ge(s.vh, 1)
    pe.transpose(T.bkA[:, 128:256], T.w_sb[:, 0:128], T.idb[:]).then_inc(s.tA, 1)
    pe.transpose(T.bkA[:, 256:384], T.w_sb[:, 128:256], T.idb[:]).then_inc(s.tA, 1)
    pe.transpose(T.bkB[:, 0:128], T.w_sb[:, 256:384], T.idb[:]).then_inc(s.tB, 1)
    pe.transpose(T.bkB[:, 128:256], T.w_sb[:, 384:512], T.idb[:]).then_inc(s.tB, 1)

    v.wait_ge(s.tH, 1)
    v.tensor_copy(T.hT[:], T.bkA[:, 0:128]).then_inc(s.vh, 1)

    v.wait_ge(s.mm1, 1)
    v.tensor_reduce(T.sta[:, 0:1], T.zT[:], AX, ALU.max, negate=True).then_inc(s.vmax, 1)
    sy.wait_ge(s.vmax, 1)
    sy.dma_start(T.la[rank], T.sta[:, 0:1]).then_inc(s.d1a, 16)
    g.wait_ge(s.d1a, 16)
    exchange(T.la[rank], s.arr_a)

    a.wait_ge(s.tA, 2)
    a.activation(T.wT[:, 0:256], T.bkA[:, 128:384], ACT.Copy).then_inc(s.acA, 1)
    v.wait_ge(s.tB, 2)
    v.tensor_copy(T.wT[:, 256:512], T.bkB[:, 0:256]).then_inc(s.vcb, 1)

    a.wait_ge(s.vmax, 1)
    a.activation(T.esc[:], T.zT[:], ACT.Exp, bias=T.sta[:, 0:1], scale=1.0,
                 accum_out=T.stb[:, 0:1]).then_inc(s.aexp, 1)

    pe.wait_ge(s.ld_oh, 16)
    pe.wait_ge(s.acA, 1)
    pe.matmul(T.U[:, 0:128], T.oh_sb[:, 0:128], T.wT[:, 0:128], True, False)
    pe.matmul(T.U[:, 0:128], T.oh_sb[:, 128:256], T.wT[:, 128:256], False, False)
    pe.wait_ge(s.vcb, 1)
    pe.matmul(T.U[:, 0:128], T.oh_sb[:, 256:384], T.wT[:, 256:384], False, False)
    pe.matmul(T.U[:, 0:128], T.oh_sb[:, 384:512], T.wT[:, 384:512], False, True).then_inc(s.mmU, 1)
    v.wait_ge(s.mmU, 1)
    v.wait_ge(s.vh, 1)
    v.tensor_tensor(T.q[:], T.U[:, 0:128], T.hT[:], ALU.mult).then_inc(s.vq, 1)
    v.wait_ge(s.vq, 1)
    v.tensor_reduce(T.stb[:, 1:2], T.q[:], AX, ALU.add).then_inc(s.vt, 1)

    sy.wait_ge(s.aexp, 1)
    sy.wait_ge(s.vt, 1)
    sy.dma_start(T.lb[rank], T.stb[:, 0:2]).then_inc(s.d1b, 16)
    g.wait_ge(s.d1b, 16)
    exchange(T.lb[rank], s.arr_b)

    a.wait_ge(s.d1a, 16)
    a.wait_ge(s.arr_a, N - 1)
    a.dma_start(T.ta[0:N, :], T.la[:]).then_inc(s.d2a, 16)
    pe.wait_ge(s.d2a, 16)
    pe.wait_ge(s.c_idn, 1)
    pe.transpose(T.p1[:, 0:N], T.ta[0:N, :], T.idn[0:N, :]).then_inc(s.t1, 1)
    v.wait_ge(s.t1, 1)
    v.tensor_reduce(T.nmn[:, 0:1], T.p1[:, 0:N], AX, ALU.min).then_inc(s.v1, 1)
    a.wait_ge(s.v1, 1)
    a.activation(T.ee[:], T.p1[:, 0:N], ACT.Exp, bias=T.nmn[:, 0:1], scale=-1.0).then_inc(s.a1, 1)

    sy.wait_ge(s.d1b, 16)
    sy.wait_ge(s.arr_b, N - 1)
    sy.dma_start(T.tb[0:N, :], T.lb[:]).then_inc(s.d2b, 16)
    pe.wait_ge(s.d2b, 16)
    pe.wait_ge(s.c_ones, 1)
    pe.transpose(T.p2[:, 0:N], T.tb[0:N, 0:2 * TK:2], T.idn[0:N, :]).then_inc(s.t2, 1)
    pe.matmul(T.p3[:, 0:1], T.tb[0:N, 1:2 * TK:2], T.ones[0:N, 0:1], True, True).then_inc(s.t3, 1)

    const = D * (K + 1) / 2 - 1.0 - D * D / 16
    v.wait_ge(s.a1, 1)
    v.wait_ge(s.t2, 1)
    v.tensor_tensor(T.pp[:], T.ee[:], T.p2[:, 0:N], ALU.mult).then_inc(s.v2, 1)
    v.wait_ge(s.v2, 1)
    v.tensor_reduce(T.ssum[:, 0:1], T.pp[:], AX, ALU.add).then_inc(s.v3, 1)
    a.wait_ge(s.v3, 1)
    a.wait_ge(s.c_thr, 1)
    a.activation(T.sgn[:], T.thr[:], ACT.Sign, bias=T.ssum[:, 0:1], scale=-1.0,
                 accum_out=T.cnt[:, 0:1]).then_inc(s.a2, 1)
    a.wait_ge(s.a2, 1)
    a.activation(T.uu[:, 0:1], T.cnt[:, 0:1], ACT.Exp, bias=-D * (K + 1) / 2, scale=-D / 2).then_inc(s.a3, 1)
    v.wait_ge(s.v1, 1)
    v.wait_ge(s.t3, 1)
    v.tensor_scalar(T.b1[:, 0:1], T.p3[:, 0:1], T.nmn[:, 0:1], -const, ALU.add, ALU.add).then_inc(s.vb, 1)
    v.wait_ge(s.a2, 1)
    v.wait_ge(s.vb, 1)
    v.tensor_scalar(T.rr[:, 0:1], T.cnt[:, 0:1], D / 2, T.b1[:, 0:1], ALU.mult, ALU.subtract).then_inc(s.v6, 1)
    v.wait_ge(s.a3, 1)
    v.wait_ge(s.v6, 1)
    v.wait_ge(s.v3, 1)
    v.tensor_scalar(T.lcol[:, 0:1], T.uu[:, 0:1], T.ssum[:, 0:1], T.rr[:, 0:1], ALU.mult, ALU.add).then_inc(s.v7, 1)

    sy.wait_ge(s.v7, 1)
    sy.dma_start(T.l[:], T.lcol[:, 0:1]).then_inc(s.d3, 16)
    sy.wait_ge(s.d3, 16)
    g.wait_ge(s.sent, 2 * NENG)
